import numpy as np
import ml_dtypes


def mxq(x, axis, fmt="e4m3"):
    dtype, down = {"e4m3": (ml_dtypes.float8_e4m3fn, 7), "e5m2": (ml_dtypes.float8_e5m2, 14)}[fmt]
    v = np.moveaxis(np.asarray(x, np.float32).astype(ml_dtypes.bfloat16).astype(np.float64), axis, -1)
    blocks = v.reshape(v.shape[:-1] + (-1, 32))
    amax = np.abs(blocks).max(-1, keepdims=True)
    byte = np.maximum(np.where(amax > 0, np.frexp(amax)[1] - 1 + 127, 0) - down, 1)
    scale = np.exp2(byte - 127.0)
    codes = (blocks / scale).astype(np.float32).astype(dtype).astype(np.float64)
    return np.moveaxis((codes * scale).reshape(v.shape), -1, axis)


WIDE = False


def mx_kscale(k):
    if not WIDE:
        return np.ones(k)
    levels = np.array([10, -10, 5, -5, 0])
    if k % 512:
        return np.exp2(np.random.permutation(np.resize(levels, k // 32))).repeat(32)
    a = np.empty((k // 512, 16))
    for p in range(k // 512):
        a[p, :8] = np.random.permutation(np.resize(levels, 8))
        for g in range(8):
            far = levels[np.abs(levels - a[p, g]) >= 10]
            a[p, g + 8] = far[np.random.randint(len(far))]
    return np.exp2(a.ravel()).repeat(32)


def f64(x):
    return np.asarray(x).astype(np.float64)


E2M1 = np.array([0.0, 0.5, 1.0, 1.5, 2.0, 3.0, 4.0, 6.0, -0.0, -0.5, -1.0, -1.5, -2.0, -3.0, -4.0, -6.0])


def pack_weight(w, fmt):
    k, n = w.shape
    w = f64(np.asarray(w, np.float32).astype(ml_dtypes.bfloat16)).reshape(k // 32, 32, n)
    amax = np.abs(w).max(1)
    if fmt == "e4m3":
        byte = np.frexp(amax)[1] - 1 + 127 - 7
    else:
        mant, ex = np.frexp(amax / 6.0)
        byte = np.where(mant > 0.5, ex, ex - 1) + 127
    byte = np.clip(np.where(amax > 0, byte, 1), 1, 254)
    scaled = (w * np.exp2(127.0 - byte)[:, None, :]).reshape(k, n).astype(np.float32)
    by_word = np.ascontiguousarray(scaled.reshape(k // 512, 128, 4, n).transpose(0, 1, 3, 2))
    if fmt == "e4m3":
        words = by_word.astype(ml_dtypes.float8_e4m3fn).view(np.uint8)
    else:
        c = by_word.astype(ml_dtypes.float4_e2m1fn).view(np.uint8) & 0xF
        words = (c[..., 0::2] | (c[..., 1::2] << 4)).reshape(k // 512, 128, 2 * n)
    return np.ascontiguousarray(words), np.ascontiguousarray(byte.astype(np.uint8).reshape(k // 512, 16, n))


def unpack_weight(words, scales, fmt):
    g, _, n = scales.shape
    words = np.ascontiguousarray(words).reshape(g, 128, n, -1)
    if fmt == "e4m3":
        vals = words.view(ml_dtypes.float8_e4m3fn).astype(np.float64)
    else:
        nib = np.empty((g, 128, n, 4), np.uint8)
        nib[..., 0::2] = words & 0xF
        nib[..., 1::2] = words >> 4
        vals = E2M1[nib]
    vals = vals * np.repeat(np.exp2(scales.astype(np.float64) - 127.0), 8, axis=1)[..., None]
    return vals.transpose(0, 1, 3, 2).reshape(g * 512, n)


def silu(v):
    return v / (1.0 + np.exp(-np.maximum(v, -700.0)))


K, M, T = 1024, 1536, 1536


def setup_inputs():
    n = np.random.standard_normal
    s = mx_kscale(K)[:, None]
    p_w4 = pack_weight(n((K, M)) / np.sqrt(K) / s, "e2m1")
    p_w8 = pack_weight(n((K, M)) / np.sqrt(K) / s, "e4m3")
    return {
        "x": (n((K, T)) * s).astype(np.float32),
        "w4_words": p_w4[0],
        "w4_scales": p_w4[1],
        "w8_words": p_w8[0],
        "w8_scales": p_w8[1],
        "b": (0.3 * n(1536)).astype(np.float32),
    }


def reference(x, w4_words, w4_scales, w8_words, w8_scales, b):
    xa_, xb_ = mxq(np.maximum(f64(x), 0.0), 0, "e4m3"), mxq(np.maximum(-f64(x), 0.0), 0, "e4m3")
    w4_ = unpack_weight(w4_words, w4_scales, "e2m1")
    w8_ = unpack_weight(w8_words, w8_scales, "e4m3")
    y = w4_.T @ xa_ + w8_.T @ xb_
    return silu(y + f64(b)[:, None])

@@ -1,0 +1,192 @@
+from contextlib import ExitStack
+
+import concourse.mybir as mybir
+
+K, M, T = 1024, 1536, 1536
+FLOPS = 2 * 2 * K * M * T
+
+F32 = mybir.dt.float32
+BF16 = mybir.dt.bfloat16
+I32 = mybir.dt.int32
+U32 = mybir.dt.uint32
+U8 = mybir.dt.uint8
+FP8X4 = mybir.dt.float8_e4m3fn_x4
+FP4X4 = mybir.dt.float4_e2m1fn_x4
+ALU = mybir.AluOpType
+ACT = mybir.ActivationFunctionType
+
+P = 128
+PACK = 4
+PASSES = K // (P * PACK)
+BANK = 512
+HALF = BANK // 2
+CHUNKS = T // BANK
+TILES = M // P
+BANKS = 8
+LEAD = (BANKS, 6, 0)
+RUN = 4
+
+
+def tile_mix_feat_fm_crelu_silu_kernel(tc, x, w4_words, w4_scales, w8_words, w8_scales, b, out):
+    nc = tc.nc
+    x_rows = x.rearrange("(a p j) t -> a p j t", a=PASSES, j=PACK)
+    w8_bytes = w8_words.rearrange("a p n i -> a p (n i)")
+    first_cols = BANKS * P
+    rest_cols = M - first_cols
+
+    with ExitStack() as ctx:
+        keep = ctx.enter_context(tc.tile_pool(name="keep", bufs=1))
+        stage = ctx.enter_context(tc.tile_pool(name="stage", bufs=4))
+        results = ctx.enter_context(tc.tile_pool(name="results", bufs=CHUNKS * TILES + 1))
+        psum = ctx.enter_context(tc.psum_pool(name="psum", bufs=BANKS))
+        ctx.enter_context(tc.manual_schedule())
+
+        bias_rows = keep.tile([P, 32], F32, name="bias_rows", align_bytes=64)
+        w4_plane = keep.tile([P, PASSES, M], U8, name="w4_plane", align_bytes=64)
+        w8_plane = keep.tile([P, M], U8, name="w8_plane", align_bytes=64)
+        nc.vector.memset(bias_rows[:], 0.0)
+        nc.vector.memset(w4_plane[:].rearrange("p a n -> p (a n)").bitcast(I32), 0)
+        nc.vector.memset(w8_plane[:].bitcast(I32), 0)
+
+        b_blocks = b.rearrange("(j q c) -> q j c", q=4, c=32)
+        for q in range(4):
+            nc.gpsimd.dma_start(out=bias_rows[32 * q : 32 * q + TILES, :], in_=b_blocks[q])
+
+        x_raw = {}
+
+        def load_x(chunk, a, col0, width):
+            raw = keep.tile([P, PACK, width], F32, name="x_raw_%d_%d_%d" % (chunk, a, col0))
+            t0 = chunk * BANK + col0
+            nc.sync.dma_start(out=raw[:], in_=x_rows[a][:, :, t0 : t0 + width])
+            x_raw[chunk, a, col0] = raw
+
+        def load_first_words(words, a, bytes_per_col, name):
+            tile = keep.tile([P, first_cols * bytes_per_col], U8, name=name, align_bytes=64)
+            nc.sync.dma_start(out=tile[:].bitcast(I32), in_=words[a][:, 0 : first_cols * bytes_per_col].bitcast(I32))
+            return tile
+
+        def load_rest_words(words, bytes_per_col, name):
+            tile = keep.tile([P, PASSES, rest_cols * bytes_per_col], U8, name=name, align_bytes=64)
+            src = words[:, :, first_cols * bytes_per_col : M * bytes_per_col].rearrange("a p n -> p a n")
+            nc.sync.dma_start(out=tile[:].bitcast(I32), in_=src.bitcast(I32))
+            return tile
+
+        w4_first, w8_first = {}, {}
+        load_x(0, 0, 0, HALF)
+        w4_first[0] = load_first_words(w4_words, 0, 2, "w4_first_0")
+        for q in range(4):
+            nc.scalar.dma_start(
+                out=w4_plane[32 * q : 32 * q + 4, :, :].bitcast(I32),
+                in_=w4_scales[:, 4 * q : 4 * q + 4, :].rearrange("a r n -> r a n").bitcast(I32),
+            )
+        load_x(0, 0, HALF, HALF)
+        for q in range(4):
+            nc.sync.dma_start(
+                out=w8_plane[32 * q + 4 : 32 * q + 12, :].bitcast(I32),
+                in_=w8_scales[:, 4 * q : 4 * q + 4, :].bitcast(I32),
+            )
+        w8_first[0] = load_first_words(w8_bytes, 0, 4, "w8_first_0")
+        load_x(0, 1, 0, HALF)
+        w4_first[1] = load_first_words(w4_words, 1, 2, "w4_first_1")
+        load_x(0, 1, HALF, HALF)
+        w8_first[1] = load_first_words(w8_bytes, 1, 4, "w8_first_1")
+        w4_rest = load_rest_words(w4_words, 2, "w4_rest")
+        w8_rest = load_rest_words(w8_bytes, 4, "w8_rest")
+        for chunk in range(1, CHUNKS):
+            for a in range(PASSES):
+                load_x(chunk, a, 0, BANK)
+
+        bias = keep.tile([P, 32], F32, name="bias", align_bytes=64)
+
+        codes, planes = {}, {}
+        for chunk in range(CHUNKS):
+            for a in range(PASSES):
+                for sign in (1, -1):
+                    label = "%d_%d_%d" % (chunk, a, sign + 1)
+                    codes[chunk, a, sign] = keep.tile([P, BANK], U32, name="x_codes_" + label, align_bytes=64)
+                    planes[chunk, a, sign] = keep.tile([P, BANK], U8, name="x_plane_" + label, align_bytes=64)
+
+        def rectify(chunk, a, sign, col0, width, on_scalar):
+            grouped = stage.tile([P, width, PACK], BF16, name="grouped", tag="grouped", align_bytes=64)
+            dst = grouped[:].rearrange("p (c i) j -> p c j i", i=RUN)
+            src = x_raw[chunk, a, col0][:].rearrange("p j (c i) -> p c j i", i=RUN)
+            if on_scalar:
+                nc.scalar.activation(out=dst, in_=src, func=ACT.Relu, scale=float(sign))
+            else:
+                nc.vector.tensor_scalar(out=dst, in0=src, scalar1=float(sign), scalar2=0.0, op0=ALU.mult, op1=ALU.max)
+            return grouped
+
+        def quantize(chunk, a, sign, col0, width, grouped):
+            nc.vector.quantize_mx(
+                out=codes[chunk, a, sign][:, col0 : col0 + width].bitcast(FP8X4),
+                scales=planes[chunk, a, sign][:, col0 : col0 + width],
+                in_=grouped[:].rearrange("p c j -> p (c j)"),
+            )
+
+        for a in range(PASSES):
+            for col0 in (0, HALF):
+                positive = rectify(0, a, 1, col0, HALF, False)
+                negative = rectify(0, a, -1, col0, HALF, True)
+                quantize(0, a, 1, col0, HALF, positive)
+                quantize(0, a, -1, col0, HALF, negative)
+            if a == 0:
+                nc.vector.transpose(bias[:], bias_rows[:])
+        for chunk in range(1, CHUNKS):
+            for a in range(PASSES):
+                positive = rectify(chunk, a, 1, 0, BANK, False)
+                negative = rectify(chunk, a, -1, 0, BANK, False)
+                quantize(chunk, a, 1, 0, BANK, positive)
+                quantize(chunk, a, -1, 0, BANK, negative)
+
+        def weights(j, a, sign):
+            cols = slice(j * P, (j + 1) * P)
+            if sign == 1:
+                first, rest, nbytes, dtype, plane = w4_first, w4_rest, 2 * P, FP4X4, w4_plane[:, a, cols]
+            else:
+                first, rest, nbytes, dtype, plane = w8_first, w8_rest, 4 * P, FP8X4, w8_plane[4 + 4 * a : P, cols]
+            if j < BANKS:
+                words = first[a][:, j * nbytes : (j + 1) * nbytes]
+            else:
+                words = rest[:, a, (j - BANKS) * nbytes : (j - BANKS + 1) * nbytes]
+            return words.bitcast(dtype), plane
+
+        def multiply(acc, chunk, j, a, sign, col0, width, start, stop):
+            words, plane = weights(j, a, sign)
+            cols = slice(col0, col0 + width)
+            nc.tensor.matmul_mx(
+                out=acc,
+                lhsT=words,
+                lhsT_scale=plane,
+                rhs=codes[chunk, a, sign][:, cols].bitcast(FP8X4),
+                rhs_scale=planes[chunk, a, sign][:, cols],
+                start=start,
+                stop=stop,
+            )
+
+        def finish(acc, chunk, j, col0, width):
+            result = results.tile([P, width], F32, name="result", tag="result")
+            nc.scalar.activation(out=result[:], in_=acc, func=ACT.Silu, bias=bias[:, j : j + 1])
+            t0 = chunk * BANK + col0
+            nc.sync.dma_start(out=out[j * P : (j + 1) * P, t0 : t0 + width], in_=result[:])
+
+        whole_steps = [(a, sign, 0, BANK) for a in range(PASSES) for sign in (1, -1)]
+        split_steps = []
+        for a in range(PASSES):
+            split_steps.extend([(a, 1, 0, HALF), (a, 1, HALF, HALF), (a, -1, 0, BANK)])
+
+        for chunk in range(CHUNKS):
+            steps = split_steps if chunk == 0 else whole_steps
+            accs = [psum.tile([P, BANK], F32, name="acc", tag="acc") for j in range(LEAD[chunk])]
+            for s, (a, sign, col0, width) in enumerate(steps):
+                last = s == len(steps) - 1
+                for j in range(LEAD[chunk]):
+                    multiply(accs[j][:, col0 : col0 + width], chunk, j, a, sign, col0, width, s == 0, last)
+                    if last:
+                        finish(accs[j][:], chunk, j, 0, BANK)
+            for j in range(LEAD[chunk], TILES):
+                final = chunk == CHUNKS - 1 and j == TILES - 1
+                for col0, width in ((0, HALF), (HALF, HALF)) if final else ((0, BANK),):
+                    acc = psum.tile([P, width], F32, name="acc", tag="acc")
+                    for s, (a, sign, unused0, unused1) in enumerate(whole_steps):
+                        multiply(acc[:], chunk, j, a, sign, col0, width, s == 0, s == len(whole_steps) - 1)
+                    finish(acc[:], chunk, j, col0, width)

@@ -23,8 +23,8 @@ HALF = BANK // 2
 CHUNKS = T // BANK
 TILES = M // P
 BANKS = 8
-LEAD = (BANKS, 6, 0)
-RUN = 4
+LEAD = (BANKS, BANKS, 4)
+RUN = 2
 
 
 def tile_mix_feat_fm_crelu_silu_kernel(tc, x, w4_words, w4_scales, w8_words, w8_scales, b, out):
@@ -37,20 +37,17 @@ def tile_mix_feat_fm_crelu_silu_kernel(tc, x, w4_words, w4_scales, w8_words, w8_
     with ExitStack() as ctx:
         keep = ctx.enter_context(tc.tile_pool(name="keep", bufs=1))
         stage = ctx.enter_context(tc.tile_pool(name="stage", bufs=4))
-        results = ctx.enter_context(tc.tile_pool(name="results", bufs=CHUNKS * TILES + 1))
+        results = ctx.enter_context(tc.tile_pool(name="results", bufs=1))
         psum = ctx.enter_context(tc.psum_pool(name="psum", bufs=BANKS))
         ctx.enter_context(tc.manual_schedule())
 
         bias_rows = keep.tile([P, 32], F32, name="bias_rows", align_bytes=64)
         w4_plane = keep.tile([P, PASSES, M], U8, name="w4_plane", align_bytes=64)
         w8_plane = keep.tile([P, M], U8, name="w8_plane", align_bytes=64)
-        nc.vector.memset(bias_rows[:], 0.0)
         nc.vector.memset(w4_plane[:].rearrange("p a n -> p (a n)").bitcast(I32), 0)
         nc.vector.memset(w8_plane[:].bitcast(I32), 0)
+        nc.vector.memset(bias_rows[:], 0.0)
 
-        b_blocks = b.rearrange("(j q c) -> q j c", q=4, c=32)
-        for q in range(4):
-            nc.gpsimd.dma_start(out=bias_rows[32 * q : 32 * q + TILES, :], in_=b_blocks[q])
 
         x_raw = {}
 
@@ -90,6 +87,9 @@ def tile_mix_feat_fm_crelu_silu_kernel(tc, x, w4_words, w4_scales, w8_words, w8_
         w4_first[1] = load_first_words(w4_words, 1, 2, "w4_first_1")
         load_x(0, 1, HALF, HALF)
         w8_first[1] = load_first_words(w8_bytes, 1, 4, "w8_first_1")
+        b_blocks = b.rearrange("(j q c) -> q j c", q=4, c=32)
+        for q in range(4):
+            nc.sync.dma_start(out=bias_rows[32 * q : 32 * q + TILES, :], in_=b_blocks[q])
         w4_rest = load_rest_words(w4_words, 2, "w4_rest")
         w8_rest = load_rest_words(w8_bytes, 4, "w8_rest")
         for chunk in range(1, CHUNKS):
@@ -129,14 +129,16 @@ def tile_mix_feat_fm_crelu_silu_kernel(tc, x, w4_words, w4_scales, w8_words, w8_
                 negative = rectify(0, a, -1, col0, HALF, True)
                 quantize(0, a, 1, col0, HALF, positive)
                 quantize(0, a, -1, col0, HALF, negative)
-            if a == 0:
-                nc.vector.transpose(bias[:], bias_rows[:])
-        for chunk in range(1, CHUNKS):
-            for a in range(PASSES):
-                positive = rectify(chunk, a, 1, 0, BANK, False)
-                negative = rectify(chunk, a, -1, 0, BANK, False)
-                quantize(chunk, a, 1, 0, BANK, positive)
-                quantize(chunk, a, -1, 0, BANK, negative)
+        nc.vector.transpose(bias[:], bias_rows[:])
+        operands = [(chunk, a, sign) for chunk in range(1, CHUNKS) for a in range(PASSES) for sign in (1, -1)]
+        first = rectify(*operands[0], 0, BANK, False)
+        quantize(*operands[0], 0, BANK, first)
+        waiting = rectify(*operands[1], 0, BANK, False)
+        for previous, operand in zip(operands[1:], operands[2:]):
+            ahead = rectify(*operand, 0, BANK, False)
+            quantize(*previous, 0, BANK, waiting)
+            waiting = ahead
+        quantize(*operands[-1], 0, BANK, waiting)
 
         def weights(j, a, sign):
             cols = slice(j * P, (j + 1) * P)
@@ -163,11 +165,21 @@ def tile_mix_feat_fm_crelu_silu_kernel(tc, x, w4_words, w4_scales, w8_words, w8_
                 stop=stop,
             )
 
+        out_pairs = out.rearrange("(g e p) t -> g p e t", e=2, p=P)
+        pairs = {}
+
         def finish(acc, chunk, j, col0, width):
-            result = results.tile([P, width], F32, name="result", tag="result")
-            nc.scalar.activation(out=result[:], in_=acc, func=ACT.Silu, bias=bias[:, j : j + 1])
-            t0 = chunk * BANK + col0
-            nc.sync.dma_start(out=out[j * P : (j + 1) * P, t0 : t0 + width], in_=result[:])
+            g, e = divmod(j, 2)
+            if (chunk, g) not in pairs:
+                pairs[chunk, g] = results.tile([P, 2, BANK], F32, name="result_%d_%d" % (chunk, g))
+            result = pairs[chunk, g]
+            nc.scalar.activation(out=result[:, e, col0 : col0 + width], in_=acc, func=ACT.Silu, bias=bias[:, j : j + 1])
+            t0 = chunk * BANK
+            if chunk == CHUNKS - 1 and g == TILES // 2 - 1:
+                cols = slice(t0 + col0, t0 + col0 + width)
+                nc.sync.dma_start(out=out_pairs[g][:, e, cols], in_=result[:, e, col0 : col0 + width])
+            elif e == 1:
+                nc.sync.dma_start(out=out_pairs[g][:, :, t0 : t0 + BANK], in_=result[:])
 
         whole_steps = [(a, sign, 0, BANK) for a in range(PASSES) for sign in (1, -1)]
         split_steps = []

from contextlib import ExitStack

import concourse.mybir as mybir

K, M, T = 1024, 1536, 1536
FLOPS = 2 * 2 * K * M * T

F32 = mybir.dt.float32
BF16 = mybir.dt.bfloat16
I32 = mybir.dt.int32
U32 = mybir.dt.uint32
U8 = mybir.dt.uint8
FP8X4 = mybir.dt.float8_e4m3fn_x4
FP4X4 = mybir.dt.float4_e2m1fn_x4
ALU = mybir.AluOpType
ACT = mybir.ActivationFunctionType

P = 128
PACK = 4
PASSES = K // (P * PACK)
BANK = 512
HALF = BANK // 2
CHUNKS = T // BANK
TILES = M // P
BANKS = 8
LEAD = (BANKS, BANKS, 4)
RUN = 2


def tile_mix_feat_fm_crelu_silu_kernel(tc, x, w4_words, w4_scales, w8_words, w8_scales, b, out):
    nc = tc.nc
    x_rows = x.rearrange("(a p j) t -> a p j t", a=PASSES, j=PACK)
    w8_bytes = w8_words.rearrange("a p n i -> a p (n i)")
    first_cols = BANKS * P
    rest_cols = M - first_cols

    with ExitStack() as ctx:
        keep = ctx.enter_context(tc.tile_pool(name="keep", bufs=1))
        stage = ctx.enter_context(tc.tile_pool(name="stage", bufs=4))
        results = ctx.enter_context(tc.tile_pool(name="results", bufs=1))
        psum = ctx.enter_context(tc.psum_pool(name="psum", bufs=BANKS))
        ctx.enter_context(tc.manual_schedule())

        bias_rows = keep.tile([P, 32], F32, name="bias_rows", align_bytes=64)
        w4_plane = keep.tile([P, PASSES, M], U8, name="w4_plane", align_bytes=64)
        w8_plane = keep.tile([P, M], U8, name="w8_plane", align_bytes=64)
        nc.vector.memset(w4_plane[:].rearrange("p a n -> p (a n)").bitcast(I32), 0)
        nc.vector.memset(w8_plane[:].bitcast(I32), 0)
        nc.vector.memset(bias_rows[:], 0.0)


        x_raw = {}

        def load_x(chunk, a, col0, width):
            raw = keep.tile([P, PACK, width], F32, name="x_raw_%d_%d_%d" % (chunk, a, col0))
            t0 = chunk * BANK + col0
            nc.sync.dma_start(out=raw[:], in_=x_rows[a][:, :, t0 : t0 + width])
            x_raw[chunk, a, col0] = raw

        def load_first_words(words, a, bytes_per_col, name):
            tile = keep.tile([P, first_cols * bytes_per_col], U8, name=name, align_bytes=64)
            nc.sync.dma_start(out=tile[:].bitcast(I32), in_=words[a][:, 0 : first_cols * bytes_per_col].bitcast(I32))
            return tile

        def load_rest_words(words, bytes_per_col, name):
            tile = keep.tile([P, PASSES, rest_cols * bytes_per_col], U8, name=name, align_bytes=64)
            src = words[:, :, first_cols * bytes_per_col : M * bytes_per_col].rearrange("a p n -> p a n")
            nc.sync.dma_start(out=tile[:].bitcast(I32), in_=src.bitcast(I32))
            return tile

        w4_first, w8_first = {}, {}
        load_x(0, 0, 0, HALF)
        w4_first[0] = load_first_words(w4_words, 0, 2, "w4_first_0")
        for q in range(4):
            nc.scalar.dma_start(
                out=w4_plane[32 * q : 32 * q + 4, :, :].bitcast(I32),
                in_=w4_scales[:, 4 * q : 4 * q + 4, :].rearrange("a r n -> r a n").bitcast(I32),
            )
        load_x(0, 0, HALF, HALF)
        for q in range(4):
            nc.sync.dma_start(
                out=w8_plane[32 * q + 4 : 32 * q + 12, :].bitcast(I32),
                in_=w8_scales[:, 4 * q : 4 * q + 4, :].bitcast(I32),
            )
        w8_first[0] = load_first_words(w8_bytes, 0, 4, "w8_first_0")
        load_x(0, 1, 0, HALF)
        w4_first[1] = load_first_words(w4_words, 1, 2, "w4_first_1")
        load_x(0, 1, HALF, HALF)
        w8_first[1] = load_first_words(w8_bytes, 1, 4, "w8_first_1")
        b_blocks = b.rearrange("(j q c) -> q j c", q=4, c=32)
        for q in range(4):
            nc.sync.dma_start(out=bias_rows[32 * q : 32 * q + TILES, :], in_=b_blocks[q])
        w4_rest = load_rest_words(w4_words, 2, "w4_rest")
        w8_rest = load_rest_words(w8_bytes, 4, "w8_rest")
        for chunk in range(1, CHUNKS):
            for a in range(PASSES):
                load_x(chunk, a, 0, BANK)

        bias = keep.tile([P, 32], F32, name="bias", align_bytes=64)

        codes, planes = {}, {}
        for chunk in range(CHUNKS):
            for a in range(PASSES):
                for sign in (1, -1):
                    label = "%d_%d_%d" % (chunk, a, sign + 1)
                    codes[chunk, a, sign] = keep.tile([P, BANK], U32, name="x_codes_" + label, align_bytes=64)
                    planes[chunk, a, sign] = keep.tile([P, BANK], U8, name="x_plane_" + label, align_bytes=64)

        def rectify(chunk, a, sign, col0, width, on_scalar):
            grouped = stage.tile([P, width, PACK], BF16, name="grouped", tag="grouped", align_bytes=64)
            dst = grouped[:].rearrange("p (c i) j -> p c j i", i=RUN)
            src = x_raw[chunk, a, col0][:].rearrange("p j (c i) -> p c j i", i=RUN)
            if on_scalar:
                nc.scalar.activation(out=dst, in_=src, func=ACT.Relu, scale=float(sign))
            else:
                nc.vector.tensor_scalar(out=dst, in0=src, scalar1=float(sign), scalar2=0.0, op0=ALU.mult, op1=ALU.max)
            return grouped

        def quantize(chunk, a, sign, col0, width, grouped):
            nc.vector.quantize_mx(
                out=codes[chunk, a, sign][:, col0 : col0 + width].bitcast(FP8X4),
                scales=planes[chunk, a, sign][:, col0 : col0 + width],
                in_=grouped[:].rearrange("p c j -> p (c j)"),
            )

        for a in range(PASSES):
            for col0 in (0, HALF):
                positive = rectify(0, a, 1, col0, HALF, False)
                negative = rectify(0, a, -1, col0, HALF, True)
                quantize(0, a, 1, col0, HALF, positive)
                quantize(0, a, -1, col0, HALF, negative)
        nc.vector.transpose(bias[:], bias_rows[:])
        operands = [(chunk, a, sign) for chunk in range(1, CHUNKS) for a in range(PASSES) for sign in (1, -1)]
        first = rectify(*operands[0], 0, BANK, False)
        quantize(*operands[0], 0, BANK, first)
        waiting = rectify(*operands[1], 0, BANK, False)
        for previous, operand in zip(operands[1:], operands[2:]):
            ahead = rectify(*operand, 0, BANK, False)
            quantize(*previous, 0, BANK, waiting)
            waiting = ahead
        quantize(*operands[-1], 0, BANK, waiting)

        def weights(j, a, sign):
            cols = slice(j * P, (j + 1) * P)
            if sign == 1:
                first, rest, nbytes, dtype, plane = w4_first, w4_rest, 2 * P, FP4X4, w4_plane[:, a, cols]
            else:
                first, rest, nbytes, dtype, plane = w8_first, w8_rest, 4 * P, FP8X4, w8_plane[4 + 4 * a : P, cols]
            if j < BANKS:
                words = first[a][:, j * nbytes : (j + 1) * nbytes]
            else:
                words = rest[:, a, (j - BANKS) * nbytes : (j - BANKS + 1) * nbytes]
            return words.bitcast(dtype), plane

        def multiply(acc, chunk, j, a, sign, col0, width, start, stop):
            words, plane = weights(j, a, sign)
            cols = slice(col0, col0 + width)
            nc.tensor.matmul_mx(
                out=acc,
                lhsT=words,
                lhsT_scale=plane,
                rhs=codes[chunk, a, sign][:, cols].bitcast(FP8X4),
                rhs_scale=planes[chunk, a, sign][:, cols],
                start=start,
                stop=stop,
            )

        out_pairs = out.rearrange("(g e p) t -> g p e t", e=2, p=P)
        pairs = {}

        def finish(acc, chunk, j, col0, width):
            g, e = divmod(j, 2)
            if (chunk, g) not in pairs:
                pairs[chunk, g] = results.tile([P, 2, BANK], F32, name="result_%d_%d" % (chunk, g))
            result = pairs[chunk, g]
            nc.scalar.activation(out=result[:, e, col0 : col0 + width], in_=acc, func=ACT.Silu, bias=bias[:, j : j + 1])
            t0 = chunk * BANK
            if chunk == CHUNKS - 1 and g == TILES // 2 - 1:
                cols = slice(t0 + col0, t0 + col0 + width)
                nc.sync.dma_start(out=out_pairs[g][:, e, cols], in_=result[:, e, col0 : col0 + width])
            elif e == 1:
                nc.sync.dma_start(out=out_pairs[g][:, :, t0 : t0 + BANK], in_=result[:])

        whole_steps = [(a, sign, 0, BANK) for a in range(PASSES) for sign in (1, -1)]
        split_steps = []
        for a in range(PASSES):
            split_steps.extend([(a, 1, 0, HALF), (a, 1, HALF, HALF), (a, -1, 0, BANK)])

        for chunk in range(CHUNKS):
            steps = split_steps if chunk == 0 else whole_steps
            accs = [psum.tile([P, BANK], F32, name="acc", tag="acc") for j in range(LEAD[chunk])]
            for s, (a, sign, col0, width) in enumerate(steps):
                last = s == len(steps) - 1
                for j in range(LEAD[chunk]):
                    multiply(accs[j][:, col0 : col0 + width], chunk, j, a, sign, col0, width, s == 0, last)
                    if last:
                        finish(accs[j][:], chunk, j, 0, BANK)
            for j in range(LEAD[chunk], TILES):
                final = chunk == CHUNKS - 1 and j == TILES - 1
                for col0, width in ((0, HALF), (HALF, HALF)) if final else ((0, BANK),):
                    acc = psum.tile([P, width], F32, name="acc", tag="acc")
                    for s, (a, sign, unused0, unused1) in enumerate(whole_steps):
                        multiply(acc[:], chunk, j, a, sign, col0, width, s == 0, s == len(whole_steps) - 1)
                    finish(acc[:], chunk, j, col0, width)
